import numpy as np, ml_dtypes
CORES = [24,48,72,152,176,200]
N = 6
import mx_ref
NC = 256
BF = ml_dtypes.bfloat16
def setup_inputs(rng):
    def f(*shape):
        return mx_ref.flush((rng.standard_normal(shape, dtype=np.float32) * np.exp2(rng.integers(-2, 3, shape[:-1] + (1,)))).astype(BF))
    return {"w": f(N, 128, 512), "x": f(N, 128, 4 * NC)}
def setup_inputs_blocks(rng):
    d = setup_inputs(rng)
    for k in ("w", "x"): d[k] = mx_ref.spread(d[k], rng, 4)
    return d
def setup_inputs_wide(rng):
    d = setup_inputs(rng)
    for k in ("w", "x"): d[k] = mx_ref.flush((d[k].astype(np.float32) * np.exp2(rng.integers(-8, 9, (N, 1, 1))).astype(np.float32)).astype(BF))
    return d
def setup_inputs_zeros(rng):
    d = setup_inputs(rng); v = d["x"].reshape(N, 128, -1, 4).copy()
    v[np.broadcast_to((rng.random((N, 1, v.shape[2], 1)) < 0.33), v.shape)] = 0
    d["x"] = v.reshape(d["x"].shape)
    return d
def reference(w, x):
    QX = [mx_ref.quantize(x[j]) for j in range(N)]
    y = np.zeros((N, 128, NC), np.float32)
    for r in range(N):
        qw = mx_ref.quantize(w[r])
        for j in range(N):
            p = mx_ref.matmul(qw, QX[j])
            y[r] = p if j == 0 else np.maximum(y[r], p)
    return {"y": y}

from concourse.bass import DstId, RemoteDMATransfer
from concourse.mybir import dt, AluOpType

N = 6
NC = 256
WC = 128
BANK = 512
SIM_CORES = 256
FAN = 2

SCRATCH = {
    "xb": ("sbuf", [128, 4 * NC], "bfloat16"),
    "wb": ("sbuf", [128, 4 * WC], "bfloat16"),
    "qw": ("sbuf", [128, WC], "float8_e4m3fn_x4"),
    "sw": ("sbuf", [128, WC], "uint8"),
    "qx": ("sbuf", [128, N * NC], "float8_e4m3fn_x4"),
    "sx": ("sbuf", [128, N * NC], "uint8"),
    "acc": ("sbuf", [128, NC], "float32"),
    "ps": ("psum", [128, N * BANK], "float32"),
}
SEMAPHORES = (["ldx", "ldw", "qxd", "qwd", "hs", "hc", "sent", "vs", "st"]
              + ["arr%d" % j for j in range(N)] + ["mm%d" % k for k in range(N)])


def _engines(mask):
    return [e for e in range(mask.bit_length()) if (mask >> e) & 1]


def _mask(engines):
    m = 0
    for e in engines:
        m |= 1 << e
    return m


def _plan(cores, topo):
    n = len(cores)

    def chipmates(c):
        return [k for k in range(SIM_CORES)
                if k != c and topo.host(k) == topo.host(c) and topo.chip(k) == topo.chip(c)]

    direct, cross, load = {}, {}, {}
    for r, c in enumerate(cores):
        others = [(r + s) % n for s in range(1, n)]
        direct[r] = [j for j in others if topo.may_write(c, cores[j])]
        cross[r] = [j for j in others if not topo.may_write(c, cores[j])]
        for j in direct[r]:
            key = (j, topo.die(c))
            load[key] = load.get(key, 0) + 1
    used, relays, turn = set(cores), {}, {}
    for r, c in enumerate(cores):
        relays[r] = []
        for i in range(0, len(cross[r]), FAN):
            group = cross[r][i:i + FAN]
            dies = sorted({topo.die(k) for k in chipmates(c)},
                          key=lambda d: (max(load.get((j, d), 0) for j in group), d != topo.die(c)))
            d = dies[0]
            h = [k for k in chipmates(c) if topo.die(k) == d and k not in used
                 and all(topo.may_write(k, cores[j]) for j in group)][0]
            used.add(h)
            orders = sorted([group, group[::-1]],
                            key=lambda o: sum(turn.get((j, d, t), 0) for t, j in enumerate(o)))
            group = orders[0]
            for t, j in enumerate(group):
                turn[(j, d, t)] = turn.get((j, d, t), 0) + 1
                load[(j, d)] = load.get((j, d), 0) + 1
            relays[r].append((h, group))
    return direct, relays


def rank_program(g, core, T, topo):
    cores = list(T.cores)
    direct, relays = _plan(cores, topo)

    def piece(kind, j):
        a, b = j * NC, (j + 1) * NC
        return T.sx[:, a:b] if kind == "s" else T.qx[:, a:b].bitcast(dt.uint8)

    def transfer(kind, j, dests, engines, sem):
        ids = []
        for d in dests:
            rid, pid = topo.addr(d, core)
            ids.append(DstId(rid=rid, pnc=pid))
        return RemoteDMATransfer(dst_ids=ids, dma_engine_mask=_mask(engines), remote_sem=sem,
                                 srcs=[piece(kind, j)], dsts=[piece(kind, j) for _ in dests])

    def lanes(c, far, near):
        out = _engines(topo.mask(c, far))
        return out, [e for e in _engines(topo.mask(c, near)) if e not in out]

    hand = {"s": T.sem.hs, "c": T.sem.hc}

    for r in range(len(cores)):
        for i, (h, group) in enumerate(relays[r]):
            if h != core:
                continue
            out, rest = lanes(cores[r], cores[direct[r][0]], h)
            got = len((rest, out)[i])
            mine = _engines(topo.mask(core, cores[group[0]]))
            for kind in ("s", "c"):
                g.wait_ge(hand[kind], got)
                g.remote_dma_fused([transfer(kind, r, [cores[j] for j in group], mine, T.sem["arr%d" % r])],
                                   local_sem=T.sem.sent)
            g.wait_ge(T.sem.sent, 2 * len(mine))
            return

    r = T.rank_of(core)
    if r is None:
        return

    g.sync.dma_start(T.xb[:], T.x[:]).then_inc(T.sem.ldx, 16)
    g.sync.dma_start(T.wb[:], T.w[:]).then_inc(T.sem.ldw, 16)
    v = g.vector
    v.wait_ge(T.sem.ldx, 16)
    v.quantize_mx(T.qx[:, r * NC:(r + 1) * NC], T.sx[:, r * NC:(r + 1) * NC], T.xb[:]).then_inc(T.sem.qxd, 1)
    v.wait_ge(T.sem.ldw, 16)
    v.quantize_mx(T.qw[:], T.sw[:], T.wb[:]).then_inc(T.sem.qwd, 1)

    out, rest = lanes(core, cores[direct[r][0]], relays[r][0][0])
    straight = [cores[j] for j in direct[r]]
    mysem = T.sem["arr%d" % r]
    both = len(relays[r]) < 2
    sent = 0
    g.wait_ge(T.sem.qxd, 1)
    for kind in ("s", "c"):
        call = [transfer(kind, r, [h], (rest, out)[i], hand[kind]) for i, (h, _) in enumerate(relays[r])]
        sent += sum(len((rest, out)[i]) for i in range(len(relays[r])))
        if both:
            call.append(transfer(kind, r, straight, out, mysem))
            sent += len(out)
        g.remote_dma_fused(call, local_sem=T.sem.sent)
    if not both:
        for kind in ("s", "c"):
            g.remote_dma_fused([transfer(kind, r, straight, out, mysem)], local_sem=T.sem.sent)
            sent += len(out)

    near = sorted((direct[j].index(r), j) for j in range(len(cores)) if r in direct[j])
    far = sorted((grp.index(r), j) for j in range(len(cores)) for _, grp in relays[j] if r in grp)
    order = [r] + [j for _, j in near] + [j for _, j in far]
    sender = {j: cores[j] for _, j in near}
    for j in range(len(cores)):
        for h, grp in relays[j]:
            if r in grp:
                sender[j] = h
    te = g.tensor
    te.wait_ge(T.sem.qwd, 1)
    te.wait_ge(T.sem.qxd, 1)
    for k, j in enumerate(order):
        if j != r:
            te.wait_ge(T.sem["arr%d" % j], 2 * len(_engines(topo.mask(sender[j], core))))
        te.matmul_mx(T.ps[:, k * BANK:k * BANK + NC], T.qw[:], T.sw[:],
                     T.qx[:, j * NC:(j + 1) * NC], T.sx[:, j * NC:(j + 1) * NC], True, True).then_inc(T.sem["mm%d" % k], 1)

    for k in range(len(order)):
        v.wait_ge(T.sem["mm%d" % k], 1)
        if k == 0:
            v.tensor_copy(T.acc[:], T.ps[:, 0:NC]).then_inc(T.sem.vs, 1)
        else:
            v.wait_ge(T.sem.vs, k)
            v.tensor_tensor(T.acc[:], T.acc[:], T.ps[:, k * BANK:k * BANK + NC], AluOpType.max).then_inc(T.sem.vs, 1)
    g.sync.wait_ge(T.sem.vs, len(order))
    g.sync.dma_start(T.y[:], T.acc[:]).then_inc(T.sem.st, 16)
    g.sync.wait_ge(T.sem.st, 16)
    g.wait_ge(T.sem.sent, sent)
